import numpy as np
import ml_dtypes


def mxq(x, axis, fmt="e4m3"):
    dtype, down = {"e4m3": (ml_dtypes.float8_e4m3fn, 7), "e5m2": (ml_dtypes.float8_e5m2, 14)}[fmt]
    v = np.moveaxis(np.asarray(x, np.float32).astype(ml_dtypes.bfloat16).astype(np.float64), axis, -1)
    blocks = v.reshape(v.shape[:-1] + (-1, 32))
    amax = np.abs(blocks).max(-1, keepdims=True)
    byte = np.maximum(np.where(amax > 0, np.frexp(amax)[1] - 1 + 127, 0) - down, 1)
    scale = np.exp2(byte - 127.0)
    codes = (blocks / scale).astype(np.float32).astype(dtype).astype(np.float64)
    return np.moveaxis((codes * scale).reshape(v.shape), -1, axis)


WIDE = False


def mx_kscale(k):
    if not WIDE:
        return np.ones(k)
    levels = np.array([10, -10, 5, -5, 0])
    if k % 512:
        return np.exp2(np.random.permutation(np.resize(levels, k // 32))).repeat(32)
    a = np.empty((k // 512, 16))
    for p in range(k // 512):
        a[p, :8] = np.random.permutation(np.resize(levels, 8))
        for g in range(8):
            far = levels[np.abs(levels - a[p, g]) >= 10]
            a[p, g + 8] = far[np.random.randint(len(far))]
    return np.exp2(a.ravel()).repeat(32)


def f64(x):
    return np.asarray(x).astype(np.float64)


def striped(idx):
    return np.tile(idx.reshape(-1, 16).T, (8, 1)).astype(np.uint16)


def unstriped(offs):
    return offs[:16].T.reshape(-1).astype(np.int64)


def striped8(idx):
    return np.concatenate([x.reshape(-1, 16).T for x in idx]).astype(np.uint16)


def runs(offs, k):
    lists = np.stack([offs[16 * r : 16 * r + 16].T.reshape(-1) for r in range(8)]).astype(np.int64)
    return lists[np.arange(k) % 512 // 64]


def pack_weight(w):
    k, n = w.shape
    w = f64(np.asarray(w, np.float32).astype(ml_dtypes.bfloat16)).reshape(k // 32, 32, n)
    amax = np.abs(w).max(1)
    byte = np.clip(np.where(amax > 0, np.frexp(amax)[1] - 1 + 127 - 7, 1), 1, 254)
    scaled = (w * np.exp2(127.0 - byte)[:, None, :]).reshape(k, n).astype(np.float32)
    words = np.ascontiguousarray(scaled.reshape(k // 512, 128, 4, n).transpose(0, 1, 3, 2)).astype(ml_dtypes.float8_e4m3fn).view(np.uint8)
    return words, np.ascontiguousarray(byte.astype(np.uint8).reshape(k // 512, 16, n))


def unpack_weight(words, scales):
    g, p, n, _ = words.shape
    vals = np.ascontiguousarray(words).view(ml_dtypes.float8_e4m3fn).astype(np.float64) * np.repeat(np.exp2(scales.astype(np.float64) - 127.0), 8, axis=1)[..., None]
    return vals.transpose(0, 1, 3, 2).reshape(g * 512, n)


E2M1 = np.array([0.0, 0.5, 1.0, 1.5, 2.0, 3.0, 4.0, 6.0, -0.0, -0.5, -1.0, -1.5, -2.0, -3.0, -4.0, -6.0])


def pack_fp4(w):
    k, n = w.shape
    w = f64(np.asarray(w, np.float32).astype(ml_dtypes.bfloat16)).reshape(k // 32, 32, n)
    amax = np.abs(w).max(1)
    mant, ex = np.frexp(amax / 6.0)
    byte = np.clip(np.where(amax > 0, np.where(mant > 0.5, ex, ex - 1) + 127, 1), 1, 254)
    scaled = (w * np.exp2(127.0 - byte)[:, None, :]).reshape(k, n).astype(np.float32)
    c = np.ascontiguousarray(scaled.reshape(k // 512, 128, 4, n).transpose(0, 1, 3, 2)).astype(ml_dtypes.float4_e2m1fn).view(np.uint8) & 0xF
    words = (c[..., 0::2] | (c[..., 1::2] << 4)).reshape(k // 512, 128, 2 * n)
    return np.ascontiguousarray(words), np.ascontiguousarray(byte.astype(np.uint8).reshape(k // 512, 16, n))


def unpack_fp4(words, scales):
    g, _, n = scales.shape
    words = np.ascontiguousarray(words).reshape(g, 128, n, 2)
    nib = np.empty((g, 128, n, 4), np.uint8)
    nib[..., 0::2] = words & 0xF
    nib[..., 1::2] = words >> 4
    vals = E2M1[nib] * np.repeat(np.exp2(scales.astype(np.float64) - 127.0), 8, axis=1)[..., None]
    return vals.transpose(0, 1, 3, 2).reshape(g * 512, n)


def planes(y):
    n, m = y.shape
    v = y.astype(np.float32).astype(ml_dtypes.bfloat16).astype(np.float64).reshape(n // 32, 32, m)
    top = np.abs(v).max(1)
    byte = np.clip(np.where(top > 0, np.frexp(top)[1] - 1 + 127 - 7, 1), 1, 254)
    codes = (v * np.exp2(127.0 - byte)[:, None, :]).reshape(n, m).astype(np.float32).astype(ml_dtypes.float8_e4m3fn).view(np.uint8)
    words = codes.reshape(n // 512, 128, 4, m).transpose(0, 1, 3, 2)
    return np.ascontiguousarray(words), np.ascontiguousarray(byte.astype(np.uint8).reshape(n // 512, 16, m))


K, T, S, H, C = 512, 2048, 512, 512, 512


def setup_inputs():
    n = np.random.standard_normal
    s = mx_kscale(K)[:, None]
    packed_xT = pack_weight(n((K, T)) * s)
    packed_w1 = pack_fp4(n((K, H)) / np.sqrt(K) / s)
    packed_w2 = pack_fp4(n((K, H)) / np.sqrt(K) / s)
    return {
        "x_words": packed_xT[0],
        "x_scales": packed_xT[1],
        "w1_words": packed_w1[0],
        "w1_scales": packed_w1[1],
        "w2_words": packed_w2[0],
        "w2_scales": packed_w2[1],
        "gs": (np.random.uniform(0.5, 1.5, (K, 1)) / s).astype(np.float32),
        "offs": striped(np.random.permutation(T)[:S]),
        "two": striped(np.random.permutation(T)[:S]),
        "n1": striped8(np.stack([np.random.permutation(S) for _ in range(8)])),
        "n2": striped8(np.stack([np.random.permutation(S) for _ in range(8)])),
        "cand": striped(np.random.permutation(T)[:C]),
        "n3": striped8(np.stack([np.random.permutation(S) for _ in range(8)])),
        "n4": striped8(np.stack([np.random.permutation(S) for _ in range(8)])),
    }


def reference(x_words, x_scales, w1_words, w1_scales, w2_words, w2_scales, gs, offs, two, n1, n2, cand, n3, n4):
    x_cand = unpack_weight(x_words, x_scales)[:, unstriped(cand)]
    xq = unpack_weight(x_words, x_scales)[:, unstriped(offs)]
    y = unpack_fp4(w1_words, w1_scales).T @ xq
    x_two = unpack_weight(x_words, x_scales)[:, unstriped(two)]
    d = unpack_fp4(w2_words, w2_scales).T @ x_two
    z = f64(gs) * (np.maximum(y, d[np.arange(H)[:, None], runs(n2, H)]) - (np.minimum(y[np.arange(H)[:, None], runs(n1, H)], d)))
    s = 0.0625 * ((x_cand.T @ mxq(z, 0, "e4m3")))
    out_0 = s[np.arange(C)[:, None], runs(n3, C)] + 0.75 * (s[np.arange(C)[:, None], runs(n4, C)])
    return (out_0,) + planes(out_0)

@@ -1,0 +1,268 @@
+from contextlib import ExitStack
+
+import concourse.mybir as mybir
+from concourse.masks import make_identity
+
+K, T, S, H, C = 512, 2048, 512, 512, 512
+FLOPS = 2 * K * H * S * 2 + 2 * H * C * S
+
+F32 = mybir.dt.float32
+BF16 = mybir.dt.bfloat16
+I32 = mybir.dt.int32
+U32 = mybir.dt.uint32
+U16 = mybir.dt.uint16
+U8 = mybir.dt.uint8
+FP8X4 = mybir.dt.float8_e4m3fn_x4
+FP4X4 = mybir.dt.float4_e2m1fn_x4
+ADD = mybir.AluOpType.add
+MULT = mybir.AluOpType.mult
+ACT = mybir.ActivationFunctionType
+
+P = 128
+PACK = 4
+LIST_ROWS = 16
+STRETCHES = ((0, 256), (256, 384), (384, 512))
+
+
+def tile_picked_twcmaxbsum_none_po_kernel(
+    tc, x_words, x_scales, w1_words, w1_scales, w2_words, w2_scales, gs,
+    offs, two, n1, n2, cand, n3, n4, out_0, out_1, out_2,
+):
+    nc = tc.nc
+    with ExitStack() as ctx:
+        lists = ctx.enter_context(tc.tile_pool(name="lists", bufs=1))
+        sb = ctx.enter_context(tc.tile_pool(name="sb", bufs=1))
+        psum = ctx.enter_context(tc.psum_pool(name="psum", bufs=1))
+
+        def sbuf(name, shape, dtype, tag=None):
+            return sb.tile(shape, dtype, name=name, tag=tag or name, align_bytes=64)
+
+        def bank(name, number, shape):
+            return psum.tile(shape, F32, name=name, tag="bank%d" % number)
+
+        def load_list(name, src):
+            tile = lists.tile([P, S // LIST_ROWS], U16, name=name)
+            nc.sync.dma_start(tile[:], src)
+            return tile
+
+        def entries(tile, lo, hi):
+            return tile[:, lo // LIST_ROWS : hi // LIST_ROWS]
+
+        def load_scales(tile, src):
+            for q in range(4):
+                nc.sync.dma_start(
+                    tile[32 * q : 32 * q + 4, :].bitcast(I32),
+                    src[0, 4 * q : 4 * q + 4, :].bitcast(I32),
+                )
+
+        def load_fp4(name, src):
+            tile = sbuf(name, [P, 2 * H], U8)
+            nc.sync.dma_start(tile[:].bitcast(I32), src[0].bitcast(I32))
+            return tile
+
+        xs = sbuf("xs", [P, T], U8)
+        nc.gpsimd.memset(xs[:].bitcast(I32), 0)
+        ws_raw = sbuf("ws_raw", [P, 2 * H], U8)
+        nc.vector.memset(ws_raw[:].bitcast(I32), 0)
+
+        offs_t = load_list("offs", offs)
+        two_t = load_list("two", two)
+        load_scales(xs[:], x_scales)
+        w1w_raw = load_fp4("w1w_raw", w1_words)
+        xw = sbuf("xw", [P, T], U32)
+        nc.sync.dma_start(xw[:].bitcast(I32), x_words[0].rearrange("p c r -> p (c r)").bitcast(I32))
+        w2w_raw = load_fp4("w2w_raw", w2_words)
+        load_scales(ws_raw[:, :H], w1_scales)
+        load_scales(ws_raw[:, H:], w2_scales)
+        gain = sbuf("gain", [P, PACK], F32)
+        nc.sync.dma_start(gain[:], gs.rearrange("(p t) o -> p (t o)", t=PACK))
+        cand_t = load_list("cand", cand)
+        n1_t = load_list("n1", n1)
+        n2_t = load_list("n2", n2)
+        n4_t = load_list("n4", n4)
+        n3_t = load_list("n3", n3)
+
+        ident = sbuf("ident", [P, P], F32)
+        make_identity(nc, ident[:])
+
+        size = sbuf("size", [P, PACK], F32)
+        nc.scalar.activation(size[:], gain[:], ACT.Abs)
+        neg_size = sbuf("neg_size", [P, PACK], F32)
+        nc.scalar.activation(neg_size[:], size[:], ACT.Copy, scale=-1.0)
+        sign = sbuf("sign", [P, PACK], BF16)
+        nc.scalar.activation(sign[:], gain[:], ACT.Sign)
+
+        def deal_bytes(name, raw, engine):
+            tile = sbuf(name, [P, PACK, P], U8)
+            engine.tensor_copy(tile[:], raw[:].rearrange("p (m t) -> p t m", t=PACK))
+            return tile
+
+        def deal_fp4(name, raw):
+            tile = sbuf(name, [P, PACK, 2 * P], U8)
+            nc.vector.tensor_copy(
+                tile[:].rearrange("p t (m b) -> p t m b", b=2),
+                raw[:].rearrange("p (m t b) -> p t m b", t=PACK, b=2),
+            )
+            return tile
+
+        xq_s = sbuf("xq_s", [P, S], U8)
+        nc.vector.tensor_copy(xq_s[:], xs[:].indirect(offs_t[:]))
+        xt_s = sbuf("xt_s", [P, S], U8)
+        nc.vector.tensor_copy(xt_s[:], xs[:].indirect(two_t[:]))
+        w1w = deal_fp4("w1w", w1w_raw)
+        xq_w = sbuf("xq_w", [P, S], U32)
+        nc.vector.tensor_copy(xq_w[:], xw[:].indirect(offs_t[:]))
+        w2w = deal_fp4("w2w", w2w_raw)
+        ws = sbuf("ws", [P, 2, PACK, P], U8)
+        nc.vector.tensor_copy(ws[:], ws_raw[:].rearrange("p (w m t) -> p w t m", w=2, t=PACK))
+        w1s, w2s = ws[:, 0, :, :], ws[:, 1, :, :]
+        xt_w = sbuf("xt_w", [P, S], U32)
+        nc.vector.tensor_copy(xt_w[:], xw[:].indirect(two_t[:]))
+        xc_raw = sbuf("xc_raw", [P, C], U8)
+        nc.vector.tensor_copy(xc_raw[:], xs[:].indirect(cand_t[:]))
+        xc_s = deal_bytes("xc_s", xc_raw, nc.vector)
+        xc_w = sbuf("xc_w", [P, PACK, P], U32)
+        nc.vector.tensor_copy(xc_w[:].rearrange("p t m -> p m t"), xw[:].indirect(cand_t[:]))
+
+        def project(out, words, scales, t, x_w, x_s, lo, hi):
+            nc.tensor.matmul_mx(
+                out, lhsT=words[:, t, :].bitcast(FP4X4), lhsT_scale=scales[:, t, :],
+                rhs=x_w[:, lo:hi].bitcast(FP8X4), rhs_scale=x_s[:, lo:hi],
+                start=True, stop=True,
+            )
+
+        y = [sbuf("y%d" % t, [P, S], F32) for t in range(PACK)]
+        nd = [sbuf("nd%d" % t, [P, S], F32) for t in range(PACK)]
+        y_ps = [bank("y_ps%d" % t, t, [P, S]) for t in range(PACK)]
+        d_ps = [bank("d_ps%d" % t, 4 + t, [P, S]) for t in range(PACK)]
+
+        def scaled(out, src, scale):
+            nc.scalar.activation(out, src, ACT.Copy, scale=scale)
+
+        for t in range(PACK):
+            project(y_ps[t][:], w1w, w1s, t, xq_w, xq_s, 0, S)
+            project(d_ps[t][:], w2w, w2s, t, xt_w, xt_s, 0, S)
+        for t in range(PACK):
+            scaled(y[t][:], y_ps[t][:], size[:, t : t + 1])
+            scaled(nd[t][:], d_ps[t][:], neg_size[:, t : t + 1])
+
+        sums = [bank("sums%d" % c, c, [P, PACK, P]) for c in range(4)]
+        for t in range(PACK):
+            for c in range(4):
+                cols = slice(c * P, (c + 1) * P)
+                nc.tensor.matmul(sums[c][:, t, :], y[t][:, cols], ident[:], start=(t == 0), stop=False, is_transpose=True)
+                nc.tensor.matmul(sums[c][:, t, :], nd[t][:, cols], ident[:], start=False, stop=False, is_transpose=True)
+
+        z_s = sbuf("z_s", [P, S], U8)
+        z_in = [sbuf("z_in%d" % g, [P, hi - lo, PACK], BF16) for g, (lo, hi) in enumerate(STRETCHES)]
+        back = {}
+
+        def compare(g, t, tag, short):
+            lo, hi = STRETCHES[g]
+            gap = sbuf("gap%d_%d" % (g, t), [P, 2, hi - lo], F32, tag=tag)
+            nc.vector.tensor_tensor(gap[:, 0, :], y[t][:].indirect(entries(n1_t, lo, hi)), nd[t][:, lo:hi], ADD)
+            nc.vector.tensor_tensor(gap[:, 1, :], nd[t][:].indirect(entries(n2_t, lo, hi)), y[t][:, lo:hi], ADD)
+            nc.scalar.activation(short, gap[:], ACT.Relu, scale=-1.0)
+            for c in range(lo // P, hi // P):
+                cols = slice(c * P - lo, (c + 1) * P - lo)
+                for i in range(2):
+                    nc.tensor.matmul(
+                        sums[c][:, t, :], short[:, i, cols], ident[:],
+                        start=False, stop=(t == PACK - 1 and i == 1), is_transpose=True,
+                    )
+            return gap
+
+        def turn_back(c):
+            pairs = sbuf("pairs%d" % c, [P, 2, P, 2], BF16)
+            nc.scalar.copy(pairs[:], sums[c][:].rearrange("n (u e) p -> n u p e", e=2))
+            words = pairs[:].rearrange("n u p e -> n u (p e)").bitcast(F32)
+            back[c] = bank("back%d" % c, c, [P, 2, P])
+            for u in range(2):
+                nc.tensor.transpose(back[c][:, u, :], words[:, u, :], ident[:])
+
+        def signed(g, c):
+            lo = STRETCHES[g][0]
+            nc.vector.tensor_tensor(
+                z_in[g][:, c * P - lo : (c + 1) * P - lo, :].rearrange("p n (u e) -> p n u e", e=2),
+                back[c][:].bitcast(BF16).rearrange("p u (n e) -> p n u e", e=2),
+                sign[:].rearrange("p (u e) -> p u e", e=2).unsqueeze(1).to_broadcast([P, P, 2, 2]),
+                MULT,
+            )
+
+        def quantise_z(g):
+            lo, hi = STRETCHES[g]
+            nc.vector.quantize_mx(
+                out=z_w[:, lo:hi].bitcast(FP8X4), scales=z_s[:, lo:hi],
+                in_=z_in[g][:].rearrange("p n t -> p (n t)"),
+            )
+
+        for t in range(PACK):
+            compare(0, t, "gap%d" % t, sbuf("short0_%d" % t, [P, 2, 2 * P], F32)[:])
+        for c in range(2):
+            turn_back(c)
+            signed(0, c)
+        early = sbuf("short1_early", [P, 2, 2, P], F32)
+        late = sbuf("short1_late", [P, 2, 2, P], F32, tag="pairs0")
+        for t in range(PACK):
+            compare(1, t, "gap%d" % t, (early, late)[t // 2][:, t % 2, :, :])
+        turn_back(2)
+        signed(1, 2)
+        early = sbuf("short2_early", [P, 3, 2, P], F32, tag="pairs1")
+        late = sbuf("short2_late", [P, 2, P], F32, tag="pairs2")
+        for t in range(PACK):
+            last = compare(2, t, "short0_%d" % t, early[:, t, :, :] if t < 3 else late[:])
+        turn_back(3)
+        z_w = sbuf("z_w", [P, S], U32, tag="pairs2")
+        quantise_z(0)
+        quantise_z(1)
+        signed(2, 3)
+        quantise_z(2)
+
+        s = [sbuf("s%d" % t, [P, S], F32) for t in range(PACK)]
+        scores = {}
+        for g, (lo, hi) in enumerate(STRETCHES):
+            n = hi - lo
+            numbers = ((4, 5), (6,), (7, 0, 1, 2))[g]
+            per_bank = PACK // len(numbers)
+            for b, number in enumerate(numbers):
+                s_ps = bank("s_ps%d_%d" % (g, b), number, [P, per_bank, n])
+                for i in range(per_bank):
+                    t = b * per_bank + i
+                    nc.tensor.matmul_mx(
+                        s_ps[:, i, :], lhsT=xc_w[:, t, :].bitcast(FP8X4), lhsT_scale=xc_s[:, t, :],
+                        rhs=z_w[:, lo:hi].bitcast(FP8X4), rhs_scale=z_s[:, lo:hi],
+                        start=True, stop=True,
+                    )
+                    scores[g, t] = s_ps[:, i, :]
+        for t in range(PACK):
+            for g, (lo, hi) in enumerate(STRETCHES):
+                scaled(s[t][:, lo:hi], scores[g, t], 0.0625)
+
+        o_w = sbuf("o_w", [P, S], U32)
+        o_s = sbuf("o_s", [P, S], U8)
+        rows = out_0.rearrange("(p t) c -> p t c", t=PACK)
+        codes = out_1[0].rearrange("p c r -> p (c r)").bitcast(I32)
+        for g, (lo, hi) in enumerate(STRETCHES):
+            n = hi - lo
+            res = sbuf("res%d" % g, [P, PACK, n], F32)
+            for t in range(PACK):
+                part = sbuf("part%d_%d" % (g, t), [P, n], F32)
+                nc.vector.tensor_scalar(part[:], s[t][:].indirect(entries(n4_t, lo, hi)), 0.75, 0.0, MULT, ADD)
+                nc.vector.tensor_tensor(res[:, t, :], s[t][:].indirect(entries(n3_t, lo, hi)), part[:], ADD)
+            nc.sync.dma_start(rows[:, :, lo:hi], res[:])
+            grouped = sbuf("o_in%d" % g, [P, n, PACK], BF16)
+            if g < len(STRETCHES) - 1:
+                nc.scalar.copy(grouped[:], res[:].rearrange("p t n -> p n t"))
+            else:
+                nc.vector.tensor_copy(grouped[:], res[:].rearrange("p t n -> p n t"))
+            nc.vector.quantize_mx(
+                out=o_w[:, lo:hi].bitcast(FP8X4), scales=o_s[:, lo:hi],
+                in_=grouped[:].rearrange("p n t -> p (n t)"),
+            )
+            nc.sync.dma_start(codes[:, lo:hi], o_w[:, lo:hi].bitcast(I32))
+        for q in range(4):
+            queue = nc.scalar if q % 2 else nc.sync
+            queue.dma_start(
+                out_2[0, 4 * q : 4 * q + 4, :].bitcast(I32),
+                o_s[32 * q : 32 * q + 4, :].bitcast(I32),
+            )

@@ -16,6 +16,7 @@ FP8X4 = mybir.dt.float8_e4m3fn_x4
 FP4X4 = mybir.dt.float4_e2m1fn_x4
 ADD = mybir.AluOpType.add
 MULT = mybir.AluOpType.mult
+MAX = mybir.AluOpType.max
 ACT = mybir.ActivationFunctionType
 
 P = 128
@@ -62,18 +63,20 @@ def tile_picked_twcmaxbsum_none_po_kernel(
 
         xs = sbuf("xs", [P, T], U8)
         nc.gpsimd.memset(xs[:].bitcast(I32), 0)
-        ws_raw = sbuf("ws_raw", [P, 2 * H], U8)
-        nc.vector.memset(ws_raw[:].bitcast(I32), 0)
+        w1s_raw = sbuf("w1s_raw", [P, H], U8)
+        w2s_raw = sbuf("w2s_raw", [P, H], U8)
+        nc.vector.memset(w1s_raw[:].bitcast(I32), 0)
+        nc.vector.memset(w2s_raw[:].bitcast(I32), 0)
 
         offs_t = load_list("offs", offs)
         two_t = load_list("two", two)
-        load_scales(xs[:], x_scales)
+        load_scales(xs, x_scales)
         w1w_raw = load_fp4("w1w_raw", w1_words)
         xw = sbuf("xw", [P, T], U32)
         nc.sync.dma_start(xw[:].bitcast(I32), x_words[0].rearrange("p c r -> p (c r)").bitcast(I32))
         w2w_raw = load_fp4("w2w_raw", w2_words)
-        load_scales(ws_raw[:, :H], w1_scales)
-        load_scales(ws_raw[:, H:], w2_scales)
+        load_scales(w1s_raw, w1_scales)
+        load_scales(w2s_raw, w2_scales)
         gain = sbuf("gain", [P, PACK], F32)
         nc.sync.dma_start(gain[:], gs.rearrange("(p t) o -> p (t o)", t=PACK))
         cand_t = load_list("cand", cand)
@@ -99,7 +102,7 @@ def tile_picked_twcmaxbsum_none_po_kernel(
 
         def deal_fp4(name, raw):
             tile = sbuf(name, [P, PACK, 2 * P], U8)
-            nc.vector.tensor_copy(
+            nc.gpsimd.tensor_copy(
                 tile[:].rearrange("p t (m b) -> p t m b", b=2),
                 raw[:].rearrange("p (m t b) -> p t m b", t=PACK, b=2),
             )
@@ -110,19 +113,16 @@ def tile_picked_twcmaxbsum_none_po_kernel(
         xt_s = sbuf("xt_s", [P, S], U8)
         nc.vector.tensor_copy(xt_s[:], xs[:].indirect(two_t[:]))
         w1w = deal_fp4("w1w", w1w_raw)
+        w1s = deal_bytes("w1s", w1s_raw, nc.vector)
         xq_w = sbuf("xq_w", [P, S], U32)
         nc.vector.tensor_copy(xq_w[:], xw[:].indirect(offs_t[:]))
         w2w = deal_fp4("w2w", w2w_raw)
-        ws = sbuf("ws", [P, 2, PACK, P], U8)
-        nc.vector.tensor_copy(ws[:], ws_raw[:].rearrange("p (w m t) -> p w t m", w=2, t=PACK))
-        w1s, w2s = ws[:, 0, :, :], ws[:, 1, :, :]
-        xt_w = sbuf("xt_w", [P, S], U32)
+        w2s = deal_bytes("w2s", w2s_raw, nc.vector)
+        xt_w = sbuf("xt_w", [P, S], U32, tag="w1s_raw")
         nc.vector.tensor_copy(xt_w[:], xw[:].indirect(two_t[:]))
         xc_raw = sbuf("xc_raw", [P, C], U8)
         nc.vector.tensor_copy(xc_raw[:], xs[:].indirect(cand_t[:]))
         xc_s = deal_bytes("xc_s", xc_raw, nc.vector)
-        xc_w = sbuf("xc_w", [P, PACK, P], U32)
-        nc.vector.tensor_copy(xc_w[:].rearrange("p t m -> p m t"), xw[:].indirect(cand_t[:]))
 
         def project(out, words, scales, t, x_w, x_s, lo, hi):
             nc.tensor.matmul_mx(
@@ -133,20 +133,20 @@ def tile_picked_twcmaxbsum_none_po_kernel(
 
         y = [sbuf("y%d" % t, [P, S], F32) for t in range(PACK)]
         nd = [sbuf("nd%d" % t, [P, S], F32) for t in range(PACK)]
-        y_ps = [bank("y_ps%d" % t, t, [P, S]) for t in range(PACK)]
-        d_ps = [bank("d_ps%d" % t, 4 + t, [P, S]) for t in range(PACK)]
+        y_banks, d_banks, sum_banks, score_banks = (0, 1, 2, 3), (2, 3, 4, 5), (6, 7, 0, 1), (2, 3, 4, 5)
 
         def scaled(out, src, scale):
             nc.scalar.activation(out, src, ACT.Copy, scale=scale)
 
         for t in range(PACK):
-            project(y_ps[t][:], w1w, w1s, t, xq_w, xq_s, 0, S)
-            project(d_ps[t][:], w2w, w2s, t, xt_w, xt_s, 0, S)
-        for t in range(PACK):
-            scaled(y[t][:], y_ps[t][:], size[:, t : t + 1])
-            scaled(nd[t][:], d_ps[t][:], neg_size[:, t : t + 1])
+            y_ps = bank("y_ps%d" % t, y_banks[t], [P, S])
+            project(y_ps[:], w1w, w1s, t, xq_w, xq_s, 0, S)
+            scaled(y[t][:], y_ps[:], size[:, t : t + 1])
+            d_ps = bank("d_ps%d" % t, d_banks[t], [P, S])
+            project(d_ps[:], w2w, w2s, t, xt_w, xt_s, 0, S)
+            scaled(nd[t][:], d_ps[:], neg_size[:, t : t + 1])
 
-        sums = [bank("sums%d" % c, c, [P, PACK, P]) for c in range(4)]
+        sums = [bank("sums%d" % c, sum_banks[c], [P, PACK, P]) for c in range(4)]
         for t in range(PACK):
             for c in range(4):
                 cols = slice(c * P, (c + 1) * P)
@@ -154,15 +154,19 @@ def tile_picked_twcmaxbsum_none_po_kernel(
                 nc.tensor.matmul(sums[c][:, t, :], nd[t][:, cols], ident[:], start=False, stop=False, is_transpose=True)
 
         z_s = sbuf("z_s", [P, S], U8)
-        z_in = [sbuf("z_in%d" % g, [P, hi - lo, PACK], BF16) for g, (lo, hi) in enumerate(STRETCHES)]
+        z_in = [sbuf("z_in%d" % h, [P, 2 * P, PACK], BF16) for h in range(2)]
         back = {}
 
-        def compare(g, t, tag, short):
+        def compare(g, t, gap):
             lo, hi = STRETCHES[g]
-            gap = sbuf("gap%d_%d" % (g, t), [P, 2, hi - lo], F32, tag=tag)
             nc.vector.tensor_tensor(gap[:, 0, :], y[t][:].indirect(entries(n1_t, lo, hi)), nd[t][:, lo:hi], ADD)
             nc.vector.tensor_tensor(gap[:, 1, :], nd[t][:].indirect(entries(n2_t, lo, hi)), y[t][:, lo:hi], ADD)
-            nc.scalar.activation(short, gap[:], ACT.Relu, scale=-1.0)
+
+        def relu(short, gap):
+            nc.scalar.activation(short, gap, ACT.Relu, scale=-1.0)
+
+        def add_up(g, t, short):
+            lo, hi = STRETCHES[g]
             for c in range(lo // P, hi // P):
                 cols = slice(c * P - lo, (c + 1) * P - lo)
                 for i in range(2):
@@ -170,73 +174,83 @@ def tile_picked_twcmaxbsum_none_po_kernel(
                         sums[c][:, t, :], short[:, i, cols], ident[:],
                         start=False, stop=(t == PACK - 1 and i == 1), is_transpose=True,
                     )
-            return gap
 
         def turn_back(c):
             pairs = sbuf("pairs%d" % c, [P, 2, P, 2], BF16)
             nc.scalar.copy(pairs[:], sums[c][:].rearrange("n (u e) p -> n u p e", e=2))
             words = pairs[:].rearrange("n u p e -> n u (p e)").bitcast(F32)
-            back[c] = bank("back%d" % c, c, [P, 2, P])
+            back[c] = bank("back%d" % c, sum_banks[c], [P, 2, P])
             for u in range(2):
                 nc.tensor.transpose(back[c][:, u, :], words[:, u, :], ident[:])
 
-        def signed(g, c):
-            lo = STRETCHES[g][0]
+        def signed(c):
             nc.vector.tensor_tensor(
-                z_in[g][:, c * P - lo : (c + 1) * P - lo, :].rearrange("p n (u e) -> p n u e", e=2),
+                z_in[c // 2][:, (c % 2) * P : (c % 2 + 1) * P, :].rearrange("p n (u e) -> p n u e", e=2),
                 back[c][:].bitcast(BF16).rearrange("p u (n e) -> p n u e", e=2),
                 sign[:].rearrange("p (u e) -> p u e", e=2).unsqueeze(1).to_broadcast([P, P, 2, 2]),
                 MULT,
             )
 
         def quantise_z(g):
-            lo, hi = STRETCHES[g]
+            lo, hi = g * 2 * P, (g + 1) * 2 * P
             nc.vector.quantize_mx(
                 out=z_w[:, lo:hi].bitcast(FP8X4), scales=z_s[:, lo:hi],
                 in_=z_in[g][:].rearrange("p n t -> p (n t)"),
             )
 
         for t in range(PACK):
-            compare(0, t, "gap%d" % t, sbuf("short0_%d" % t, [P, 2, 2 * P], F32)[:])
+            gap = sbuf("gap0_%d" % t, [P, 2, 2 * P], F32)
+            short = sbuf("short0_%d" % t, [P, 2, 2 * P], F32)
+            compare(0, t, gap)
+            relu(short[:], gap[:])
+            add_up(0, t, short)
         for c in range(2):
             turn_back(c)
-            signed(0, c)
-        early = sbuf("short1_early", [P, 2, 2, P], F32)
-        late = sbuf("short1_late", [P, 2, 2, P], F32, tag="pairs0")
-        for t in range(PACK):
-            compare(1, t, "gap%d" % t, (early, late)[t // 2][:, t % 2, :, :])
+            signed(c)
+
+        def two_tiles(g, first, gaps, short):
+            for t in (first, first + 1):
+                compare(g, t, gaps[:, t, :, :])
+            relu(short[:], gaps[:, first : first + 2, :, :])
+            for t in (first, first + 1):
+                add_up(g, t, short[:, t - first, :, :])
+
+        gaps = sbuf("gap1", [P, PACK, 2, P], F32, tag="gap0_0")
+        two_tiles(1, 0, gaps, sbuf("short1_early", [P, 2, 2, P], F32))
+        two_tiles(1, 2, gaps, sbuf("short1_late", [P, 2, 2, P], F32, tag="pairs0"))
         turn_back(2)
-        signed(1, 2)
+        signed(2)
+        gaps = sbuf("gap2", [P, 3, 2, P], F32, tag="gap0_1")
         early = sbuf("short2_early", [P, 3, 2, P], F32, tag="pairs1")
-        late = sbuf("short2_late", [P, 2, P], F32, tag="pairs2")
-        for t in range(PACK):
-            last = compare(2, t, "short0_%d" % t, early[:, t, :, :] if t < 3 else late[:])
+        two_tiles(2, 0, gaps, early[:, 0:2, :, :])
+        compare(2, 2, gaps[:, 2, :, :])
+        relu(early[:, 2, :, :], gaps[:, 2, :, :])
+        add_up(2, 2, early[:, 2, :, :])
+        last = sbuf("gap_last", [P, 2, P], F32, tag="gap0_2")
+        late = sbuf("short2_late", [P, 2, P], F32)
+        compare(2, 3, last)
+        nc.vector.tensor_scalar(late[:], last[:], -1.0, 0.0, MULT, MAX)
+        add_up(2, 3, late)
+        xc_w = sbuf("xc_w", [P, PACK, P], U32, tag="gap0_2")
+        nc.vector.tensor_copy(xc_w[:].rearrange("p t m -> p m t"), xw[:].indirect(cand_t[:]))
         turn_back(3)
-        z_w = sbuf("z_w", [P, S], U32, tag="pairs2")
+        z_w = sbuf("z_w", [P, S], U32, tag="short2_late")
         quantise_z(0)
+        signed(3)
         quantise_z(1)
-        signed(2, 3)
-        quantise_z(2)
 
         s = [sbuf("s%d" % t, [P, S], F32) for t in range(PACK)]
-        scores = {}
-        for g, (lo, hi) in enumerate(STRETCHES):
-            n = hi - lo
-            numbers = ((4, 5), (6,), (7, 0, 1, 2))[g]
-            per_bank = PACK // len(numbers)
-            for b, number in enumerate(numbers):
-                s_ps = bank("s_ps%d_%d" % (g, b), number, [P, per_bank, n])
-                for i in range(per_bank):
-                    t = b * per_bank + i
-                    nc.tensor.matmul_mx(
-                        s_ps[:, i, :], lhsT=xc_w[:, t, :].bitcast(FP8X4), lhsT_scale=xc_s[:, t, :],
-                        rhs=z_w[:, lo:hi].bitcast(FP8X4), rhs_scale=z_s[:, lo:hi],
-                        start=True, stop=True,
-                    )
-                    scores[g, t] = s_ps[:, i, :]
+        s_ps = [bank("s_ps%d" % t, score_banks[t], [P, S]) for t in range(PACK)]
+        for h in range(2):
+            lo, hi = h * 2 * P, (h + 1) * 2 * P
+            for t in range(PACK):
+                nc.tensor.matmul_mx(
+                    s_ps[t][:, lo:hi], lhsT=xc_w[:, t, :].bitcast(FP8X4), lhsT_scale=xc_s[:, t, :],
+                    rhs=z_w[:, lo:hi].bitcast(FP8X4), rhs_scale=z_s[:, lo:hi],
+                    start=True, stop=True,
+                )
         for t in range(PACK):
-            for g, (lo, hi) in enumerate(STRETCHES):
-                scaled(s[t][:, lo:hi], scores[g, t], 0.0625)
+            scaled(s[t][:], s_ps[t][:], 0.0625)
 
         o_w = sbuf("o_w", [P, S], U32)
         o_s = sbuf("o_s", [P, S], U8)

@@ -120,7 +120,7 @@ def tile_picked_twcmaxbsum_none_po_kernel(
         w2s = deal_bytes("w2s", w2s_raw, nc.vector)
         xt_w = sbuf("xt_w", [P, S], U32, tag="w1s_raw")
         nc.vector.tensor_copy(xt_w[:], xw[:].indirect(two_t[:]))
-        xc_raw = sbuf("xc_raw", [P, C], U8)
+        xc_raw = sbuf("xc_raw", [P, C], U8, tag="w2s_raw")
         nc.vector.tensor_copy(xc_raw[:], xs[:].indirect(cand_t[:]))
         xc_s = deal_bytes("xc_s", xc_raw, nc.vector)
 
@@ -220,30 +220,27 @@ def tile_picked_twcmaxbsum_none_po_kernel(
         two_tiles(1, 2, gaps, sbuf("short1_late", [P, 2, 2, P], F32, tag="pairs0"))
         turn_back(2)
         signed(2)
-        gaps = sbuf("gap2", [P, 3, 2, P], F32, tag="gap0_1")
-        early = sbuf("short2_early", [P, 3, 2, P], F32, tag="pairs1")
-        two_tiles(2, 0, gaps, early[:, 0:2, :, :])
-        compare(2, 2, gaps[:, 2, :, :])
-        relu(early[:, 2, :, :], gaps[:, 2, :, :])
-        add_up(2, 2, early[:, 2, :, :])
-        last = sbuf("gap_last", [P, 2, P], F32, tag="gap0_2")
-        late = sbuf("short2_late", [P, 2, P], F32)
-        compare(2, 3, last)
-        nc.vector.tensor_scalar(late[:], last[:], -1.0, 0.0, MULT, MAX)
-        add_up(2, 3, late)
-        xc_w = sbuf("xc_w", [P, PACK, P], U32, tag="gap0_2")
+        gaps = sbuf("gap2", [P, 2, 2, P], F32, tag="gap0_1")
+        two_tiles(2, 0, gaps, sbuf("short2_early", [P, 2, 2, P], F32, tag="pairs1"))
+        for t in (2, 3):
+            gap = sbuf("gap2_%d" % t, [P, 2, P], F32, tag="gap0_%d" % t)
+            short = sbuf("short2_%d" % t, [P, 2, P], F32)
+            compare(2, t, gap)
+            nc.vector.tensor_scalar(short[:], gap[:], -1.0, 0.0, MULT, MAX)
+            add_up(2, t, short)
+        xc_w = sbuf("xc_w", [P, PACK, P], U32, tag="gap0_3")
         nc.vector.tensor_copy(xc_w[:].rearrange("p t m -> p m t"), xw[:].indirect(cand_t[:]))
         turn_back(3)
-        z_w = sbuf("z_w", [P, S], U32, tag="short2_late")
-        quantise_z(0)
+        z_w = sbuf("z_w", [P, S], U32, tag="pairs3")
         signed(3)
+        quantise_z(0)
         quantise_z(1)
 
         s = [sbuf("s%d" % t, [P, S], F32) for t in range(PACK)]
         s_ps = [bank("s_ps%d" % t, score_banks[t], [P, S]) for t in range(PACK)]
-        for h in range(2):
-            lo, hi = h * 2 * P, (h + 1) * 2 * P
-            for t in range(PACK):
+        for t in range(PACK):
+            for h in range(2):
+                lo, hi = h * 2 * P, (h + 1) * 2 * P
                 nc.tensor.matmul_mx(
                     s_ps[t][:, lo:hi], lhsT=xc_w[:, t, :].bitcast(FP8X4), lhsT_scale=xc_s[:, t, :],
                     rhs=z_w[:, lo:hi].bitcast(FP8X4), rhs_scale=z_s[:, lo:hi],
@@ -256,22 +253,25 @@ def tile_picked_twcmaxbsum_none_po_kernel(
         o_s = sbuf("o_s", [P, S], U8)
         rows = out_0.rearrange("(p t) c -> p t c", t=PACK)
         codes = out_1[0].rearrange("p c r -> p (c r)").bitcast(I32)
-        for g, (lo, hi) in enumerate(STRETCHES):
-            n = hi - lo
-            res = sbuf("res%d" % g, [P, PACK, n], F32)
-            for t in range(PACK):
-                part = sbuf("part%d_%d" % (g, t), [P, n], F32)
-                nc.vector.tensor_scalar(part[:], s[t][:].indirect(entries(n4_t, lo, hi)), 0.75, 0.0, MULT, ADD)
-                nc.vector.tensor_tensor(res[:, t, :], s[t][:].indirect(entries(n3_t, lo, hi)), part[:], ADD)
-            nc.sync.dma_start(rows[:, :, lo:hi], res[:])
-            grouped = sbuf("o_in%d" % g, [P, n, PACK], BF16)
-            if g < len(STRETCHES) - 1:
-                nc.scalar.copy(grouped[:], res[:].rearrange("p t n -> p n t"))
-            else:
-                nc.vector.tensor_copy(grouped[:], res[:].rearrange("p t n -> p n t"))
+        half = S // 2
+        halves = [(h * half, (h + 1) * half) for h in range(2)]
+        res = [sbuf("res%d" % h, [P, PACK, half], F32) for h in range(2)]
+        for t in range(PACK):
+            parts = [sbuf("part%d_%d" % (h, t), [P, half], F32) for h in range(2)]
+            for h, (lo, hi) in enumerate(halves):
+                nc.vector.tensor_scalar(parts[h][:], s[t][:].indirect(entries(n4_t, lo, hi)), 0.75, 0.0, MULT, ADD)
+            for h, (lo, hi) in enumerate(halves):
+                nc.vector.tensor_tensor(res[h][:, t, :], s[t][:].indirect(entries(n3_t, lo, hi)), parts[h][:], ADD)
+                if t >= PACK - 2:
+                    first = 0 if t == PACK - 2 else t
+                    nc.sync.dma_start(rows[:, first : t + 1, lo:hi], res[h][:, first : t + 1, :])
+        grouped = [sbuf("o_in%d" % h, [P, half, PACK], BF16) for h in range(2)]
+        nc.scalar.copy(grouped[0][:], res[0][:].rearrange("p t n -> p n t"))
+        nc.vector.tensor_copy(grouped[1][:], res[1][:].rearrange("p t n -> p n t"))
+        for h, (lo, hi) in enumerate(halves):
             nc.vector.quantize_mx(
                 out=o_w[:, lo:hi].bitcast(FP8X4), scales=o_s[:, lo:hi],
-                in_=grouped[:].rearrange("p n t -> p (n t)"),
+                in_=grouped[h][:].rearrange("p n t -> p (n t)"),
             )
             nc.sync.dma_start(codes[:, lo:hi], o_w[:, lo:hi].bitcast(I32))
         for q in range(4):

@@ -133,7 +133,7 @@ def tile_picked_twcmaxbsum_none_po_kernel(
 
         y = [sbuf("y%d" % t, [P, S], F32) for t in range(PACK)]
         nd = [sbuf("nd%d" % t, [P, S], F32) for t in range(PACK)]
-        y_banks, d_banks, sum_banks, score_banks = (0, 1, 2, 3), (2, 3, 4, 5), (6, 7, 0, 1), (2, 3, 4, 5)
+        y_banks, d_banks, sum_banks, back_banks = (0, 1, 2, 3), (2, 3, 4, 5), (6, 7, 0, 1), (6, 7, 0, 6)
 
         def scaled(out, src, scale):
             nc.scalar.activation(out, src, ACT.Copy, scale=scale)
@@ -154,7 +154,8 @@ def tile_picked_twcmaxbsum_none_po_kernel(
                 nc.tensor.matmul(sums[c][:, t, :], nd[t][:, cols], ident[:], start=False, stop=False, is_transpose=True)
 
         z_s = sbuf("z_s", [P, S], U8)
-        z_in = [sbuf("z_in%d" % h, [P, 2 * P, PACK], BF16) for h in range(2)]
+        z_w = sbuf("z_w", [P, S], U32)
+        z_in = [sbuf("z_in%d" % g, [P, hi - lo, PACK], BF16) for g, (lo, hi) in enumerate(STRETCHES)]
         back = {}
 
         def compare(g, t, gap):
@@ -177,22 +178,26 @@ def tile_picked_twcmaxbsum_none_po_kernel(
 
         def turn_back(c):
             pairs = sbuf("pairs%d" % c, [P, 2, P, 2], BF16)
-            nc.scalar.copy(pairs[:], sums[c][:].rearrange("n (u e) p -> n u p e", e=2))
+            nc.scalar.copy(
+                pairs[:].rearrange("n u (q i) e -> n u q e i", i=2),
+                sums[c][:].rearrange("n (u e) (q i) -> n u q e i", e=2, i=2),
+            )
             words = pairs[:].rearrange("n u p e -> n u (p e)").bitcast(F32)
-            back[c] = bank("back%d" % c, sum_banks[c], [P, 2, P])
+            back[c] = bank("back%d" % c, back_banks[c], [P, 2, P])
             for u in range(2):
                 nc.tensor.transpose(back[c][:, u, :], words[:, u, :], ident[:])
 
-        def signed(c):
+        def signed(g, c):
+            lo = STRETCHES[g][0]
             nc.vector.tensor_tensor(
-                z_in[c // 2][:, (c % 2) * P : (c % 2 + 1) * P, :].rearrange("p n (u e) -> p n u e", e=2),
+                z_in[g][:, c * P - lo : (c + 1) * P - lo, :].rearrange("p n (u e) -> p n u e", e=2),
                 back[c][:].bitcast(BF16).rearrange("p u (n e) -> p n u e", e=2),
                 sign[:].rearrange("p (u e) -> p u e", e=2).unsqueeze(1).to_broadcast([P, P, 2, 2]),
                 MULT,
             )
 
         def quantise_z(g):
-            lo, hi = g * 2 * P, (g + 1) * 2 * P
+            lo, hi = STRETCHES[g]
             nc.vector.quantize_mx(
                 out=z_w[:, lo:hi].bitcast(FP8X4), scales=z_s[:, lo:hi],
                 in_=z_in[g][:].rearrange("p n t -> p (n t)"),
@@ -206,7 +211,7 @@ def tile_picked_twcmaxbsum_none_po_kernel(
             add_up(0, t, short)
         for c in range(2):
             turn_back(c)
-            signed(c)
+            signed(0, c)
 
         def two_tiles(g, first, gaps, short):
             for t in (first, first + 1):
@@ -219,7 +224,7 @@ def tile_picked_twcmaxbsum_none_po_kernel(
         two_tiles(1, 0, gaps, sbuf("short1_early", [P, 2, 2, P], F32))
         two_tiles(1, 2, gaps, sbuf("short1_late", [P, 2, 2, P], F32, tag="pairs0"))
         turn_back(2)
-        signed(2)
+        signed(1, 2)
         gaps = sbuf("gap2", [P, 2, 2, P], F32, tag="gap0_1")
         two_tiles(2, 0, gaps, sbuf("short2_early", [P, 2, 2, P], F32, tag="pairs1"))
         for t in (2, 3):
@@ -230,24 +235,33 @@ def tile_picked_twcmaxbsum_none_po_kernel(
             add_up(2, t, short)
         xc_w = sbuf("xc_w", [P, PACK, P], U32, tag="gap0_3")
         nc.vector.tensor_copy(xc_w[:].rearrange("p t m -> p m t"), xw[:].indirect(cand_t[:]))
-        turn_back(3)
-        z_w = sbuf("z_w", [P, S], U32, tag="pairs3")
-        signed(3)
         quantise_z(0)
         quantise_z(1)
+        turn_back(3)
+        signed(2, 3)
+        quantise_z(2)
 
         s = [sbuf("s%d" % t, [P, S], F32) for t in range(PACK)]
-        s_ps = [bank("s_ps%d" % t, score_banks[t], [P, S]) for t in range(PACK)]
-        for t in range(PACK):
-            for h in range(2):
-                lo, hi = h * 2 * P, (h + 1) * 2 * P
-                nc.tensor.matmul_mx(
-                    s_ps[t][:, lo:hi], lhsT=xc_w[:, t, :].bitcast(FP8X4), lhsT_scale=xc_s[:, t, :],
-                    rhs=z_w[:, lo:hi].bitcast(FP8X4), rhs_scale=z_s[:, lo:hi],
-                    start=True, stop=True,
-                )
-        for t in range(PACK):
-            scaled(s[t][:], s_ps[t][:], 0.0625)
+
+        def score(out, t, lo, hi):
+            nc.tensor.matmul_mx(
+                out, lhsT=xc_w[:, t, :].bitcast(FP8X4), lhsT_scale=xc_s[:, t, :],
+                rhs=z_w[:, lo:hi].bitcast(FP8X4), rhs_scale=z_s[:, lo:hi],
+                start=True, stop=True,
+            )
+
+        edge = STRETCHES[-1][0]
+        early = bank("s_early", sum_banks[3], [P, edge])
+        for lo, hi in STRETCHES[:-1]:
+            score(early[:, lo:hi], 0, lo, hi)
+        scaled(s[0][:, :edge], early[:], 0.0625)
+        late = bank("s_late", 2, [P, S - edge])
+        score(late[:], 0, edge, S)
+        scaled(s[0][:, edge:], late[:], 0.0625)
+        for t in range(1, PACK):
+            s_ps = bank("s_ps%d" % t, 2 + t, [P, S])
+            score(s_ps[:], t, 0, S)
+            scaled(s[t][:], s_ps[:], 0.0625)
 
         o_w = sbuf("o_w", [P, S], U32)
         o_s = sbuf("o_s", [P, S], U8)
@@ -266,8 +280,11 @@ def tile_picked_twcmaxbsum_none_po_kernel(
                     first = 0 if t == PACK - 2 else t
                     nc.sync.dma_start(rows[:, first : t + 1, lo:hi], res[h][:, first : t + 1, :])
         grouped = [sbuf("o_in%d" % h, [P, half, PACK], BF16) for h in range(2)]
-        nc.scalar.copy(grouped[0][:], res[0][:].rearrange("p t n -> p n t"))
-        nc.vector.tensor_copy(grouped[1][:], res[1][:].rearrange("p t n -> p n t"))
+        for h, copy in enumerate((nc.scalar.copy, nc.vector.tensor_copy)):
+            copy(
+                grouped[h][:].rearrange("p (c i) t -> p c t i", i=4),
+                res[h][:].rearrange("p t (c i) -> p c t i", i=4),
+            )
         for h, (lo, hi) in enumerate(halves):
             nc.vector.quantize_mx(
                 out=o_w[:, lo:hi].bitcast(FP8X4), scales=o_s[:, lo:hi],

from contextlib import ExitStack

import concourse.mybir as mybir
from concourse.masks import make_identity

K, T, S, H, C = 512, 2048, 512, 512, 512
FLOPS = 2 * K * H * S * 2 + 2 * H * C * S

F32 = mybir.dt.float32
BF16 = mybir.dt.bfloat16
I32 = mybir.dt.int32
U32 = mybir.dt.uint32
U16 = mybir.dt.uint16
U8 = mybir.dt.uint8
FP8X4 = mybir.dt.float8_e4m3fn_x4
FP4X4 = mybir.dt.float4_e2m1fn_x4
ADD = mybir.AluOpType.add
MULT = mybir.AluOpType.mult
MAX = mybir.AluOpType.max
ACT = mybir.ActivationFunctionType

P = 128
PACK = 4
LIST_ROWS = 16
STRETCHES = ((0, 256), (256, 384), (384, 512))


def tile_picked_twcmaxbsum_none_po_kernel(
    tc, x_words, x_scales, w1_words, w1_scales, w2_words, w2_scales, gs,
    offs, two, n1, n2, cand, n3, n4, out_0, out_1, out_2,
):
    nc = tc.nc
    with ExitStack() as ctx:
        lists = ctx.enter_context(tc.tile_pool(name="lists", bufs=1))
        sb = ctx.enter_context(tc.tile_pool(name="sb", bufs=1))
        psum = ctx.enter_context(tc.psum_pool(name="psum", bufs=1))

        def sbuf(name, shape, dtype, tag=None):
            return sb.tile(shape, dtype, name=name, tag=tag or name, align_bytes=64)

        def bank(name, number, shape):
            return psum.tile(shape, F32, name=name, tag="bank%d" % number)

        def load_list(name, src):
            tile = lists.tile([P, S // LIST_ROWS], U16, name=name)
            nc.sync.dma_start(tile[:], src)
            return tile

        def entries(tile, lo, hi):
            return tile[:, lo // LIST_ROWS : hi // LIST_ROWS]

        def load_scales(tile, src):
            for q in range(4):
                nc.sync.dma_start(
                    tile[32 * q : 32 * q + 4, :].bitcast(I32),
                    src[0, 4 * q : 4 * q + 4, :].bitcast(I32),
                )

        def load_fp4(name, src):
            tile = sbuf(name, [P, 2 * H], U8)
            nc.sync.dma_start(tile[:].bitcast(I32), src[0].bitcast(I32))
            return tile

        xs = sbuf("xs", [P, T], U8)
        nc.gpsimd.memset(xs[:].bitcast(I32), 0)
        w1s_raw = sbuf("w1s_raw", [P, H], U8)
        w2s_raw = sbuf("w2s_raw", [P, H], U8)
        nc.vector.memset(w1s_raw[:].bitcast(I32), 0)
        nc.vector.memset(w2s_raw[:].bitcast(I32), 0)

        offs_t = load_list("offs", offs)
        two_t = load_list("two", two)
        load_scales(xs, x_scales)
        w1w_raw = load_fp4("w1w_raw", w1_words)
        xw = sbuf("xw", [P, T], U32)
        nc.sync.dma_start(xw[:].bitcast(I32), x_words[0].rearrange("p c r -> p (c r)").bitcast(I32))
        w2w_raw = load_fp4("w2w_raw", w2_words)
        load_scales(w1s_raw, w1_scales)
        load_scales(w2s_raw, w2_scales)
        gain = sbuf("gain", [P, PACK], F32)
        nc.sync.dma_start(gain[:], gs.rearrange("(p t) o -> p (t o)", t=PACK))
        cand_t = load_list("cand", cand)
        n1_t = load_list("n1", n1)
        n2_t = load_list("n2", n2)
        n4_t = load_list("n4", n4)
        n3_t = load_list("n3", n3)

        ident = sbuf("ident", [P, P], F32)
        make_identity(nc, ident[:])

        size = sbuf("size", [P, PACK], F32)
        nc.scalar.activation(size[:], gain[:], ACT.Abs)
        neg_size = sbuf("neg_size", [P, PACK], F32)
        nc.scalar.activation(neg_size[:], size[:], ACT.Copy, scale=-1.0)
        sign = sbuf("sign", [P, PACK], BF16)
        nc.scalar.activation(sign[:], gain[:], ACT.Sign)

        def deal_bytes(name, raw, engine):
            tile = sbuf(name, [P, PACK, P], U8)
            engine.tensor_copy(tile[:], raw[:].rearrange("p (m t) -> p t m", t=PACK))
            return tile

        def deal_fp4(name, raw):
            tile = sbuf(name, [P, PACK, 2 * P], U8)
            nc.gpsimd.tensor_copy(
                tile[:].rearrange("p t (m b) -> p t m b", b=2),
                raw[:].rearrange("p (m t b) -> p t m b", t=PACK, b=2),
            )
            return tile

        xq_s = sbuf("xq_s", [P, S], U8)
        nc.vector.tensor_copy(xq_s[:], xs[:].indirect(offs_t[:]))
        xt_s = sbuf("xt_s", [P, S], U8)
        nc.vector.tensor_copy(xt_s[:], xs[:].indirect(two_t[:]))
        w1w = deal_fp4("w1w", w1w_raw)
        w1s = deal_bytes("w1s", w1s_raw, nc.vector)
        xq_w = sbuf("xq_w", [P, S], U32)
        nc.vector.tensor_copy(xq_w[:], xw[:].indirect(offs_t[:]))
        w2w = deal_fp4("w2w", w2w_raw)
        w2s = deal_bytes("w2s", w2s_raw, nc.vector)
        xt_w = sbuf("xt_w", [P, S], U32, tag="w1s_raw")
        nc.vector.tensor_copy(xt_w[:], xw[:].indirect(two_t[:]))
        xc_raw = sbuf("xc_raw", [P, C], U8, tag="w2s_raw")
        nc.vector.tensor_copy(xc_raw[:], xs[:].indirect(cand_t[:]))
        xc_s = deal_bytes("xc_s", xc_raw, nc.vector)

        def project(out, words, scales, t, x_w, x_s, lo, hi):
            nc.tensor.matmul_mx(
                out, lhsT=words[:, t, :].bitcast(FP4X4), lhsT_scale=scales[:, t, :],
                rhs=x_w[:, lo:hi].bitcast(FP8X4), rhs_scale=x_s[:, lo:hi],
                start=True, stop=True,
            )

        y = [sbuf("y%d" % t, [P, S], F32) for t in range(PACK)]
        nd = [sbuf("nd%d" % t, [P, S], F32) for t in range(PACK)]
        y_banks, d_banks, sum_banks, back_banks = (0, 1, 2, 3), (2, 3, 4, 5), (6, 7, 0, 1), (6, 7, 0, 6)

        def scaled(out, src, scale):
            nc.scalar.activation(out, src, ACT.Copy, scale=scale)

        for t in range(PACK):
            y_ps = bank("y_ps%d" % t, y_banks[t], [P, S])
            project(y_ps[:], w1w, w1s, t, xq_w, xq_s, 0, S)
            scaled(y[t][:], y_ps[:], size[:, t : t + 1])
            d_ps = bank("d_ps%d" % t, d_banks[t], [P, S])
            project(d_ps[:], w2w, w2s, t, xt_w, xt_s, 0, S)
            scaled(nd[t][:], d_ps[:], neg_size[:, t : t + 1])

        sums = [bank("sums%d" % c, sum_banks[c], [P, PACK, P]) for c in range(4)]
        for t in range(PACK):
            for c in range(4):
                cols = slice(c * P, (c + 1) * P)
                nc.tensor.matmul(sums[c][:, t, :], y[t][:, cols], ident[:], start=(t == 0), stop=False, is_transpose=True)
                nc.tensor.matmul(sums[c][:, t, :], nd[t][:, cols], ident[:], start=False, stop=False, is_transpose=True)

        z_s = sbuf("z_s", [P, S], U8)
        z_w = sbuf("z_w", [P, S], U32)
        z_in = [sbuf("z_in%d" % g, [P, hi - lo, PACK], BF16) for g, (lo, hi) in enumerate(STRETCHES)]
        back = {}

        def compare(g, t, gap):
            lo, hi = STRETCHES[g]
            nc.vector.tensor_tensor(gap[:, 0, :], y[t][:].indirect(entries(n1_t, lo, hi)), nd[t][:, lo:hi], ADD)
            nc.vector.tensor_tensor(gap[:, 1, :], nd[t][:].indirect(entries(n2_t, lo, hi)), y[t][:, lo:hi], ADD)

        def relu(short, gap):
            nc.scalar.activation(short, gap, ACT.Relu, scale=-1.0)

        def add_up(g, t, short):
            lo, hi = STRETCHES[g]
            for c in range(lo // P, hi // P):
                cols = slice(c * P - lo, (c + 1) * P - lo)
                for i in range(2):
                    nc.tensor.matmul(
                        sums[c][:, t, :], short[:, i, cols], ident[:],
                        start=False, stop=(t == PACK - 1 and i == 1), is_transpose=True,
                    )

        def turn_back(c):
            pairs = sbuf("pairs%d" % c, [P, 2, P, 2], BF16)
            nc.scalar.copy(
                pairs[:].rearrange("n u (q i) e -> n u q e i", i=2),
                sums[c][:].rearrange("n (u e) (q i) -> n u q e i", e=2, i=2),
            )
            words = pairs[:].rearrange("n u p e -> n u (p e)").bitcast(F32)
            back[c] = bank("back%d" % c, back_banks[c], [P, 2, P])
            for u in range(2):
                nc.tensor.transpose(back[c][:, u, :], words[:, u, :], ident[:])

        def signed(g, c):
            lo = STRETCHES[g][0]
            nc.vector.tensor_tensor(
                z_in[g][:, c * P - lo : (c + 1) * P - lo, :].rearrange("p n (u e) -> p n u e", e=2),
                back[c][:].bitcast(BF16).rearrange("p u (n e) -> p n u e", e=2),
                sign[:].rearrange("p (u e) -> p u e", e=2).unsqueeze(1).to_broadcast([P, P, 2, 2]),
                MULT,
            )

        def quantise_z(g):
            lo, hi = STRETCHES[g]
            nc.vector.quantize_mx(
                out=z_w[:, lo:hi].bitcast(FP8X4), scales=z_s[:, lo:hi],
                in_=z_in[g][:].rearrange("p n t -> p (n t)"),
            )

        for t in range(PACK):
            gap = sbuf("gap0_%d" % t, [P, 2, 2 * P], F32)
            short = sbuf("short0_%d" % t, [P, 2, 2 * P], F32)
            compare(0, t, gap)
            relu(short[:], gap[:])
            add_up(0, t, short)
        for c in range(2):
            turn_back(c)
            signed(0, c)

        def two_tiles(g, first, gaps, short):
            for t in (first, first + 1):
                compare(g, t, gaps[:, t, :, :])
            relu(short[:], gaps[:, first : first + 2, :, :])
            for t in (first, first + 1):
                add_up(g, t, short[:, t - first, :, :])

        gaps = sbuf("gap1", [P, PACK, 2, P], F32, tag="gap0_0")
        two_tiles(1, 0, gaps, sbuf("short1_early", [P, 2, 2, P], F32))
        two_tiles(1, 2, gaps, sbuf("short1_late", [P, 2, 2, P], F32, tag="pairs0"))
        turn_back(2)
        signed(1, 2)
        gaps = sbuf("gap2", [P, 2, 2, P], F32, tag="gap0_1")
        two_tiles(2, 0, gaps, sbuf("short2_early", [P, 2, 2, P], F32, tag="pairs1"))
        for t in (2, 3):
            gap = sbuf("gap2_%d" % t, [P, 2, P], F32, tag="gap0_%d" % t)
            short = sbuf("short2_%d" % t, [P, 2, P], F32)
            compare(2, t, gap)
            nc.vector.tensor_scalar(short[:], gap[:], -1.0, 0.0, MULT, MAX)
            add_up(2, t, short)
        xc_w = sbuf("xc_w", [P, PACK, P], U32, tag="gap0_3")
        nc.vector.tensor_copy(xc_w[:].rearrange("p t m -> p m t"), xw[:].indirect(cand_t[:]))
        quantise_z(0)
        quantise_z(1)
        turn_back(3)
        signed(2, 3)
        quantise_z(2)

        s = [sbuf("s%d" % t, [P, S], F32) for t in range(PACK)]

        def score(out, t, lo, hi):
            nc.tensor.matmul_mx(
                out, lhsT=xc_w[:, t, :].bitcast(FP8X4), lhsT_scale=xc_s[:, t, :],
                rhs=z_w[:, lo:hi].bitcast(FP8X4), rhs_scale=z_s[:, lo:hi],
                start=True, stop=True,
            )

        edge = STRETCHES[-1][0]
        early = bank("s_early", sum_banks[3], [P, edge])
        for lo, hi in STRETCHES[:-1]:
            score(early[:, lo:hi], 0, lo, hi)
        scaled(s[0][:, :edge], early[:], 0.0625)
        late = bank("s_late", 2, [P, S - edge])
        score(late[:], 0, edge, S)
        scaled(s[0][:, edge:], late[:], 0.0625)
        for t in range(1, PACK):
            s_ps = bank("s_ps%d" % t, 2 + t, [P, S])
            score(s_ps[:], t, 0, S)
            scaled(s[t][:], s_ps[:], 0.0625)

        o_w = sbuf("o_w", [P, S], U32)
        o_s = sbuf("o_s", [P, S], U8)
        rows = out_0.rearrange("(p t) c -> p t c", t=PACK)
        codes = out_1[0].rearrange("p c r -> p (c r)").bitcast(I32)
        half = S // 2
        halves = [(h * half, (h + 1) * half) for h in range(2)]
        res = [sbuf("res%d" % h, [P, PACK, half], F32) for h in range(2)]
        for t in range(PACK):
            parts = [sbuf("part%d_%d" % (h, t), [P, half], F32) for h in range(2)]
            for h, (lo, hi) in enumerate(halves):
                nc.vector.tensor_scalar(parts[h][:], s[t][:].indirect(entries(n4_t, lo, hi)), 0.75, 0.0, MULT, ADD)
            for h, (lo, hi) in enumerate(halves):
                nc.vector.tensor_tensor(res[h][:, t, :], s[t][:].indirect(entries(n3_t, lo, hi)), parts[h][:], ADD)
                if t >= PACK - 2:
                    first = 0 if t == PACK - 2 else t
                    nc.sync.dma_start(rows[:, first : t + 1, lo:hi], res[h][:, first : t + 1, :])
        grouped = [sbuf("o_in%d" % h, [P, half, PACK], BF16) for h in range(2)]
        for h, copy in enumerate((nc.scalar.copy, nc.vector.tensor_copy)):
            copy(
                grouped[h][:].rearrange("p (c i) t -> p c t i", i=4),
                res[h][:].rearrange("p t (c i) -> p c t i", i=4),
            )
        for h, (lo, hi) in enumerate(halves):
            nc.vector.quantize_mx(
                out=o_w[:, lo:hi].bitcast(FP8X4), scales=o_s[:, lo:hi],
                in_=grouped[h][:].rearrange("p n t -> p (n t)"),
            )
            nc.sync.dma_start(codes[:, lo:hi], o_w[:, lo:hi].bitcast(I32))
        for q in range(4):
            queue = nc.scalar if q % 2 else nc.sync
            queue.dma_start(
                out_2[0, 4 * q : 4 * q + 4, :].bitcast(I32),
                o_s[32 * q : 32 * q + 4, :].bitcast(I32),
            )
